import numpy as np
import ml_dtypes


def mxq(x, axis, fmt="e4m3"):
    dtype, down = {"e4m3": (ml_dtypes.float8_e4m3fn, 7), "e5m2": (ml_dtypes.float8_e5m2, 14)}[fmt]
    v = np.moveaxis(np.asarray(x, np.float32).astype(ml_dtypes.bfloat16).astype(np.float64), axis, -1)
    blocks = v.reshape(v.shape[:-1] + (-1, 32))
    amax = np.abs(blocks).max(-1, keepdims=True)
    byte = np.maximum(np.where(amax > 0, np.frexp(amax)[1] - 1 + 127, 0) - down, 1)
    scale = np.exp2(byte - 127.0)
    codes = (blocks / scale).astype(np.float32).astype(dtype).astype(np.float64)
    return np.moveaxis((codes * scale).reshape(v.shape), -1, axis)


WIDE = False


def mx_kscale(k):
    if not WIDE:
        return np.ones(k)
    levels = np.array([10, -10, 5, -5, 0])
    if k % 512:
        return np.exp2(np.random.permutation(np.resize(levels, k // 32))).repeat(32)
    a = np.empty((k // 512, 16))
    for p in range(k // 512):
        a[p, :8] = np.random.permutation(np.resize(levels, 8))
        for g in range(8):
            far = levels[np.abs(levels - a[p, g]) >= 10]
            a[p, g + 8] = far[np.random.randint(len(far))]
    return np.exp2(a.ravel()).repeat(32)


BF16 = ml_dtypes.bfloat16


def bf(x):
    return np.asarray(x, np.float32).astype(BF16)


def f64(x):
    return np.asarray(x).astype(np.float64)


E2M1 = np.array([0.0, 0.5, 1.0, 1.5, 2.0, 3.0, 4.0, 6.0, -0.0, -0.5, -1.0, -1.5, -2.0, -3.0, -4.0, -6.0])


def pack_weight(w, fmt):
    k, n = w.shape
    w = f64(bf(w)).reshape(k // 32, 32, n)
    amax = np.abs(w).max(1)
    if fmt == "e4m3":
        byte = np.frexp(amax)[1] - 1 + 127 - 7
    else:
        mant, ex = np.frexp(amax / 6.0)
        byte = np.where(mant > 0.5, ex, ex - 1) + 127
    byte = np.clip(np.where(amax > 0, byte, 1), 1, 254)
    scaled = (w * np.exp2(127.0 - byte)[:, None, :]).reshape(k, n).astype(np.float32)
    by_word = np.ascontiguousarray(scaled.reshape(k // 512, 128, 4, n).transpose(0, 1, 3, 2))
    if fmt == "e4m3":
        words = by_word.astype(ml_dtypes.float8_e4m3fn).view(np.uint8)
    else:
        c = by_word.astype(ml_dtypes.float4_e2m1fn).view(np.uint8) & 0xF
        words = c[..., 0::2] | (c[..., 1::2] << 4)
    return np.ascontiguousarray(words), np.ascontiguousarray(byte.astype(np.uint8).reshape(k // 512, 16, n))


def unpack_weight(words, scales, fmt):
    g, p, n, _ = words.shape
    if fmt == "e4m3":
        vals = np.ascontiguousarray(words).view(ml_dtypes.float8_e4m3fn).astype(np.float64)
    else:
        nib = np.empty((g, p, n, 4), np.uint8)
        nib[..., 0::2] = words & 0xF
        nib[..., 1::2] = words >> 4
        vals = E2M1[nib]
    vals = vals * np.repeat(np.exp2(scales.astype(np.float64) - 127.0), 8, axis=1)[..., None]
    return vals.transpose(0, 1, 3, 2).reshape(g * 512, n)
def pack4(w):
    words, scales = pack_weight(w, "e2m1")
    return words.reshape(words.shape[0], 128, -1), scales


def unpack4(words, scales):
    return unpack_weight(words.reshape(words.shape[0], 128, -1, 2), scales, "e2m1")


T, IN, R, OUT = 1024, 2048, 512, 1536


def draw0():
    s = mx_kscale(R)
    t = mx_kscale(IN)
    x = np.random.standard_normal((T, IN)) / np.sqrt(IN)
    x_words, x_scales = pack4(x.T / t[:, None])
    a = np.random.standard_normal((IN, R)) / np.sqrt(R) * s * t[:, None]
    bmat = np.random.standard_normal((R, OUT)) / s[:, None]
    w0 = np.random.standard_normal((IN, OUT)) * t[:, None]
    return {"x_words": x_words,
            "x_scales": x_scales,
            "a": bf(a),
            "bmat": bf(bmat),
            "d_gain": bf(1 + 0.3 * np.random.standard_normal(R)),
            "b_gain": bf(1 + 0.3 * np.random.standard_normal(OUT)),
            "w0": bf(w0)}


def core(x_words, x_scales, a, bmat, d_gain, b_gain, w0):
    xt = unpack4(x_words, x_scales)
    ad = f64(a) * f64(d_gain)
    delta = mxq(ad, 1, "e4m3") @ mxq(f64(bmat), 0, "e4m3")
    wm = f64(w0) + delta * f64(b_gain)
    y = xt.T @ mxq(wm, 0, "e4m3")
    return y


def e4m3fn_bytes(y):
    return np.clip(np.asarray(y, np.float64), -448.0, 448.0).astype(np.float32).astype(ml_dtypes.float8_e4m3fn).view(np.uint8)


def e4m3fn_values(b):
    return np.asarray(b, np.uint8).view(ml_dtypes.float8_e4m3fn).astype(np.float64)


def setup_inputs():
    d = draw0()
    x0 = np.asarray(d['bmat']).astype(np.float64)
    s = (np.max(np.abs(x0), axis=(1,), keepdims=True) / 448.0).astype(np.float32)
    out = {}
    for k, v in d.items():
        if k == 'bmat':
            out['bmat_bytes'] = e4m3fn_bytes(x0 / s.astype(np.float64))
            out['bmat_scale'] = s
        else:
            out[k] = v
    return out


def reference(x_words, x_scales, a, bmat_bytes, bmat_scale, d_gain, b_gain, w0):
    return core(x_words, x_scales, a, e4m3fn_values(bmat_bytes) * bmat_scale.astype(np.float64), d_gain, b_gain, w0)

@@ -1,0 +1,393 @@
+from contextlib import ExitStack
+
+import concourse.mybir as mybir
+from concourse.masks import make_identity
+
+F32 = mybir.dt.float32
+BF16 = mybir.dt.bfloat16
+I32 = mybir.dt.int32
+U32 = mybir.dt.uint32
+U8 = mybir.dt.uint8
+E4M3 = mybir.dt.float8_e4m3fn
+E4M3X4 = mybir.dt.float8_e4m3fn_x4
+E2M1X4 = mybir.dt.float4_e2m1fn_x4
+MULT = mybir.AluOpType.mult
+ADD = mybir.AluOpType.add
+COPY = mybir.ActivationFunctionType.Copy
+
+T, IN, R, OUT = 1024, 2048, 512, 1536
+P = 128
+PACK = 4
+GROUPS = IN // (P * PACK)
+CHUNK = 512
+CHUNKS = OUT // CHUNK
+HALF = 256
+BLOCKS = OUT // P
+T_TILES = T // P
+
+FLOPS = 2 * IN * R * OUT + 2 * T * IN * OUT
+
+PANELS = [[0, 1], [2, 3], [4, 5, 6, 7], [8, 9], [10], [11]]
+PATTERNS = ["TTTT", "TTTT", "TTPP"] + ["TTPP", "PPTP"] * 4 + ["PPPP"]
+BPREP = {0: 1, 1: 2, 2: 3, 4: 4, 6: 5}
+DP, DT, TB, YB = 2, 2, 2, 2
+HP = 64
+
+
+def tile_vera_merged_layer_s13_kernel(tc, x_words, x_scales, a, bmat_bytes, bmat_scale, d_gain, b_gain, w0, out):
+    nc = tc.nc
+    with ExitStack() as ctx:
+        keep = ctx.enter_context(tc.tile_pool(name="keep", bufs=1))
+        work = ctx.enter_context(tc.tile_pool(name="work", bufs=2))
+        psum = ctx.enter_context(tc.psum_pool(name="psum", bufs=2))
+
+        d_row = keep.tile([P, R], BF16, name="d_row")
+        b_row = keep.tile([P, OUT], BF16, name="b_row")
+        ones = keep.tile([P, P], BF16, name="ones")
+        warm = keep.tile([P, 8], F32, name="warm")
+        ident = keep.tile([P, P], F32, name="ident")
+        b_sc = keep.tile([P, PACK], F32, name="b_sc")
+        b_raw = keep.tile([P, PACK, OUT], U8, name="b_raw", align_bytes=64)
+        b_wide = keep.tile([P, PACK, OUT], BF16, name="b_wide", align_bytes=64)
+        b_grp = keep.tile([P, OUT, PACK], BF16, name="b_grp", align_bytes=64)
+        b_cod = keep.tile([P, OUT], U32, name="b_cod", align_bytes=64)
+        b_pla = keep.tile([P, OUT], U8, name="b_pla", align_bytes=64)
+        a_raw = keep.tile([P, GROUPS, PACK, R], BF16, name="a_raw", align_bytes=64)
+        a_cod = keep.tile([P, GROUPS, P * PACK], U32, name="a_cod", align_bytes=64)
+        a_pla = keep.tile([P, GROUPS, P * PACK], U8, name="a_pla", align_bytes=64)
+        w_raw = keep.tile([P, GROUPS, PACK, OUT], BF16, name="w_raw", align_bytes=64)
+        w_cod = keep.tile([P, GROUPS * OUT], U32, name="w_cod", align_bytes=64)
+        w_pla = keep.tile([P, GROUPS * OUT], U8, name="w_pla", align_bytes=64)
+        x_cod = keep.tile([P, GROUPS, 2 * T], U8, name="x_cod", align_bytes=64)
+        x_pla = keep.tile([P, GROUPS, T], U8, name="x_pla", align_bytes=64)
+        dg = keep.tile([P, R], BF16, name="dg")
+        bg = keep.tile([P, OUT], F32, name="bg")
+        b_col = keep.tile([P, BLOCKS], F32, name="b_col")
+
+        a_view = a.rearrange("(g p t) r -> g p t r", p=P, t=PACK)
+        w_view = w0.rearrange("(g p t) o -> g p t o", p=P, t=PACK)
+        b_view = bmat_bytes.rearrange("(p t) o -> p t o", t=PACK)
+
+        nc.vector.memset(d_row[:], 0.0)
+        nc.scalar.dma_start(out=d_row[0:1, :], in_=d_gain.rearrange("(o r) -> o r", o=1))
+        nc.vector.memset(warm[:], 0.0)
+        nc.scalar.activation(out=warm[:, 0:4], in_=warm[:, 4:8], func=COPY)
+        nc.vector.memset(ones[:], 1.0)
+        nc.gpsimd.memset(b_row[:], 0.0)
+        nc.scalar.dma_start(out=b_row[0:1, :], in_=b_gain.rearrange("(o r) -> o r", o=1))
+        make_identity(nc, ident[:])
+        nc.gpsimd.memset(x_pla[:].rearrange("p g n -> p (g n)").bitcast(U32), 0)
+
+        nc.sync.dma_start(out=b_sc[:], in_=bmat_scale.rearrange("(p t) o -> p (t o)", t=PACK))
+        nc.sync.dma_start(out=b_raw[:, :, 0:CHUNK], in_=b_view[:, :, 0:CHUNK])
+        for h in range(2):
+            nc.sync.dma_start(out=a_raw[:, 0, 2 * h : 2 * h + 2, :], in_=a_view[0][:, 2 * h : 2 * h + 2, :])
+
+        def load_a(g):
+            nc.sync.dma_start(out=a_raw[:, g, :, :], in_=a_view[g])
+
+        def load_w(c, g):
+            cols = slice(c * CHUNK, (c + 1) * CHUNK)
+            nc.sync.dma_start(out=w_raw[:, g, :, cols], in_=w_view[g][:, :, cols])
+
+        load_a(1)
+        load_w(0, 0)
+        load_a(2)
+        load_w(0, 1)
+        load_a(3)
+        load_w(0, 2)
+        load_w(0, 3)
+        nc.sync.dma_start(out=b_raw[:, :, CHUNK:OUT], in_=b_view[:, :, CHUNK:OUT])
+        for g in range(GROUPS):
+            load_w(1, g)
+        nc.sync.dma_start(out=x_cod[:].bitcast(I32), in_=x_words.bitcast(I32).rearrange("g p n -> p g n"))
+        for q in range(4):
+            nc.sync.dma_start(
+                out=x_pla[32 * q : 32 * q + 4, :, :].bitcast(I32),
+                in_=x_scales[:, 4 * q : 4 * q + 4, :].bitcast(I32).rearrange("g q n -> q g n"),
+            )
+        for g in range(GROUPS):
+            load_w(2, g)
+
+        ad_tiles = {}
+        grp_tiles = {}
+
+        def ad_product(g, h):
+            if h == 0:
+                ad_tiles[g] = work.tile([P, PACK, R], BF16, name="ad", tag="ad", align_bytes=64)
+            ts = slice(2 * h, 2 * h + 2)
+            nc.vector.tensor_tensor(
+                out=ad_tiles[g][:, ts, :], in0=a_raw[:, g, ts, :], in1=dg[:].unsqueeze(1).to_broadcast([P, 2, R]), op=MULT
+            )
+
+        def ad_turn(g, h):
+            if h == 0:
+                grp_tiles[g] = work.tile([P, P * PACK, PACK], BF16, name="ad_grp", tag="ad_grp", align_bytes=64)
+            bank = psum.tile([P, 2, 2, P], F32, name="bank_a", tag="y", bufs=YB)
+            for s in range(2):
+                words = ad_tiles[g][:, 2 * h + s, :].bitcast(F32)
+                for u in range(2):
+                    nc.tensor.transpose(bank[:, s, u, :], words[:, u::2], ident[:])
+            nc.scalar.copy(
+                out=grp_tiles[g][:, h * HALF : (h + 1) * HALF, :].bitcast(F32).rearrange("p (s i) u -> p s i u", s=2),
+                in_=bank[:].rearrange("p s u i -> p s i u"),
+            )
+
+        def ad_quantise(g):
+            nc.vector.quantize_mx(
+                out=a_cod[:, g, :].bitcast(E4M3X4), scales=a_pla[:, g, :], in_=grp_tiles[g][:].rearrange("p n t -> p (n t)")
+            )
+
+        def b_widen(k):
+            cols = slice(k * HALF, (k + 1) * HALF)
+            for t in range(PACK):
+                nc.scalar.activation(out=b_wide[:, t, cols], in_=b_raw[:, t, cols].bitcast(E4M3), func=COPY, scale=b_sc[:, t : t + 1])
+
+        def b_interleave(k, copy):
+            cols = slice(k * HALF, (k + 1) * HALF)
+            copy(out=b_grp[:, cols, :], in_=b_wide[:, :, cols].rearrange("p t c -> p c t"))
+
+        def b_quantise(k):
+            cols = slice(k * HALF, (k + 1) * HALF)
+            nc.vector.quantize_mx(
+                out=b_cod[:, cols].bitcast(E4M3X4), scales=b_pla[:, cols], in_=b_grp[:, cols, :].rearrange("p c t -> p (c t)")
+            )
+
+        periods = []
+        last_period = {}
+        bases = {}
+        base = 0
+        for pi, panel in enumerate(PANELS):
+            bases[pi] = base
+            order = [(g, ob) for g in range(GROUPS) for ob in panel]
+            for i in range(0, len(order), 4):
+                periods.append((order[i : i + 4], base + i * P, PATTERNS[len(periods)]))
+            last_period[len(periods) - 1] = pi
+            base += GROUPS * len(panel) * P
+        banks, scaled, turned, prods, wm = {}, {}, {}, {}, {}
+
+        def first_product(k, u):
+            (g, ob), kind = periods[k][0][u], periods[k][2][u]
+            cols = slice(ob * P, (ob + 1) * P)
+            bank = psum.tile([P, PACK, P], F32, name="bank_d", tag="dt" if kind == "T" else "dp", bufs=DT if kind == "T" else DP)
+            banks[(k, u)] = bank
+            if kind == "T":
+                nc.tensor.matmul_mx(
+                    out=bank[:].rearrange("p t o -> p (t o)"),
+                    lhsT=b_cod[:, cols].bitcast(E4M3X4),
+                    lhsT_scale=b_pla[:, cols],
+                    rhs=a_cod[:, g, :].bitcast(E4M3X4),
+                    rhs_scale=a_pla[:, g, :],
+                    start=True,
+                    stop=True,
+                )
+                tile = work.tile([P, PACK, P], F32, name="scaled", tag="scaled", bufs=6)
+                scaled[(k, u)] = tile
+                nc.scalar.activation(out=tile[:], in_=bank[:], func=COPY, scale=b_col[:, ob : ob + 1])
+            else:
+                for t in range(PACK):
+                    nc.tensor.matmul_mx(
+                        out=bank[:, t, :],
+                        lhsT=a_cod[:, g, t * P : (t + 1) * P].bitcast(E4M3X4),
+                        lhsT_scale=a_pla[:, g, t * P : (t + 1) * P],
+                        rhs=b_cod[:, cols].bitcast(E4M3X4),
+                        rhs_scale=b_pla[:, cols],
+                        start=True,
+                        stop=True,
+                    )
+
+        def turn_back(k, u):
+            if periods[k][2][u] == "T":
+                bank = psum.tile([P, PACK, P], F32, name="bank_t", tag="t", bufs=TB)
+                turned[(k, u)] = bank
+                for t in range(PACK):
+                    nc.tensor.transpose(bank[:, t, :], scaled[(k, u)][:, t, :], ident[:])
+
+        def scale_plain(k, u):
+            g, ob = periods[k][0][u]
+            nc.vector.tensor_tensor(
+                out=prods[k][:, u * P : (u + 1) * P, :],
+                in0=banks[(k, u)][:].rearrange("p t o -> p o t"),
+                in1=bg[:, ob * P : (ob + 1) * P].unsqueeze(2).to_broadcast([P, P, PACK]),
+                op=MULT,
+            )
+
+        def add_turned(k, u):
+            g, ob = periods[k][0][u]
+            nc.vector.tensor_tensor(
+                out=wm[k][:, u * P : (u + 1) * P, :],
+                in0=turned[(k, u)][:].rearrange("p t o -> p o t"),
+                in1=w_raw[:, g, :, ob * P : (ob + 1) * P].rearrange("p t o -> p o t"),
+                op=ADD,
+            )
+
+        def add_plain(engine, k, lo, hi):
+            g, ob = periods[k][0][lo // P]
+            o0 = ob * P + lo % P
+            engine.tensor_tensor(
+                out=wm[k][:, lo:hi, :],
+                in0=prods[k][:, lo:hi, :],
+                in1=w_raw[:, g, :, o0 : o0 + hi - lo].rearrange("p t o -> p o t"),
+                op=ADD,
+            )
+
+        def plain_runs(k):
+            units, at, pattern = periods[k]
+            runs = []
+            for u in range(4):
+                if pattern[u] not in "Pg":
+                    continue
+                lo = u * P + (HP if pattern[u] == "g" else 0)
+                hi = (u + 1) * P
+                if runs and runs[-1][1] == lo and units[u][0] == units[u - 1][0]:
+                    runs[-1][1] = hi
+                else:
+                    runs.append([lo, hi])
+            return runs
+
+        def wm_quantise(k, lo=0, hi=4 * P):
+            at = periods[k][1]
+            nc.vector.quantize_mx(
+                out=w_cod[:, at + lo : at + hi].bitcast(E4M3X4),
+                scales=w_pla[:, at + lo : at + hi],
+                in_=wm[k][:, lo:hi, :].rearrange("p o t -> p (o t)"),
+            )
+
+        y_banks = {}
+
+        def y_product(pi, j):
+            width = len(PANELS[pi]) * P
+            n = min(width, CHUNK) if width == CHUNK else P
+            tiles = CHUNK // width
+            bank = psum.tile([P, tiles, width], F32, name="bank_y", tag="y", bufs=YB)
+            y_banks[(pi, j)] = bank
+            for i in range(tiles):
+                tt = j * tiles + i
+                for o in range(0, width, n):
+                    for g in range(GROUPS):
+                        at = bases[pi] + g * width + o
+                        nc.tensor.matmul_mx(
+                            out=bank[:, i, o : o + n],
+                            lhsT=x_cod[:, g, tt * 2 * P : (tt + 1) * 2 * P].bitcast(E2M1X4),
+                            lhsT_scale=x_pla[:, g, tt * P : (tt + 1) * P],
+                            rhs=w_cod[:, at : at + n].bitcast(E4M3X4),
+                            rhs_scale=w_pla[:, at : at + n],
+                            start=g == 0,
+                            stop=g == GROUPS - 1,
+                        )
+
+        out_view = out.rearrange("(m p) o -> p m o", p=P)
+
+        def y_store(pi, j, engine=None):
+            width = len(PANELS[pi]) * P
+            tiles = CHUNK // width
+            o0 = PANELS[pi][0] * P
+            res = work.tile([P, tiles, width], F32, name="res", tag="res", bufs=6)
+            if engine is None:
+                nc.scalar.copy(out=res[:], in_=y_banks[(pi, j)][:])
+            else:
+                engine(out=res[:], in_=y_banks[(pi, j)][:])
+            nc.sync.dma_start(out=out_view[:, j * tiles : (j + 1) * tiles, o0 : o0 + width], in_=res[:])
+
+        def b_widen_v(k):
+            cols = slice(k * HALF, (k + 1) * HALF)
+            for t in range(PACK):
+                nc.vector.tensor_scalar(
+                    out=b_wide[:, t, cols], in0=b_raw[:, t, cols].bitcast(E4M3), scalar1=b_sc[:, t : t + 1], scalar2=None, op0=MULT
+                )
+
+        bank = psum.tile([P, R], F32, name="bank_g", tag="y", bufs=YB)
+        nc.tensor.matmul(bank[:], lhsT=ones[:], rhs=d_row[:], start=True, stop=True)
+        nc.scalar.copy(out=dg[:], in_=bank[:])
+        b_widen_v(0)
+        ad_product(0, 0)
+        ad_product(0, 1)
+        ad_turn(0, 0)
+        ad_turn(0, 1)
+        bank = psum.tile([P, BLOCKS], F32, name="bank_c", tag="y", bufs=YB)
+        for ob in range(BLOCKS):
+            nc.tensor.matmul(bank[:, ob : ob + 1], lhsT=b_row[:, ob * P : (ob + 1) * P], rhs=ones[:, 0:1], start=True, stop=True)
+        b_interleave(0, nc.vector.tensor_copy)
+        ad_product(1, 0)
+        ad_product(1, 1)
+        b_quantise(0)
+        ad_quantise(0)
+        ad_turn(1, 0)
+        ad_turn(1, 1)
+        nc.scalar.copy(out=b_col[:], in_=bank[:])
+        for u in range(2):
+            first_product(0, u)
+        ad_product(2, 0)
+        ad_product(2, 1)
+        for u in range(2):
+            turn_back(0, u)
+        ad_quantise(1)
+        ad_turn(2, 0)
+        ad_turn(2, 1)
+        for u in range(2, 4):
+            first_product(0, u)
+        for u in range(2, 4):
+            turn_back(0, u)
+        ad_product(3, 0)
+        ad_product(3, 1)
+        ad_quantise(2)
+        ad_turn(3, 0)
+        ad_turn(3, 1)
+        for j in range(3):
+            bank = psum.tile([P, CHUNK], F32, name="bank_b", tag="y", bufs=YB)
+            nc.tensor.matmul(bank[:], lhsT=ones[:], rhs=b_row[:, j * CHUNK : (j + 1) * CHUNK], start=True, stop=True)
+            nc.scalar.copy(out=bg[:, j * CHUNK : (j + 1) * CHUNK], in_=bank[:])
+
+        n = len(periods)
+        todo = []
+        open_item = None
+        for k in range(n + 1):
+            if k < n:
+                units, at, pattern = periods[k]
+                prods[k] = work.tile([P, 4 * P, PACK], F32, name="prod", tag="prod", bufs=2)
+                wm[k] = work.tile([P, 4 * P, PACK], BF16, name="wm", tag="wm", bufs=3, align_bytes=64)
+                for kind in "GgP":
+                    for u in range(4):
+                        if pattern[u] == kind:
+                            scale_plain(k, u)
+                for u in range(4):
+                    if pattern[u] == "G":
+                        add_plain(nc.gpsimd, k, u * P, (u + 1) * P)
+                    if pattern[u] == "g":
+                        add_plain(nc.gpsimd, k, u * P, u * P + HP)
+                for u in range(4):
+                    if pattern[u] == "T":
+                        add_turned(k, u)
+            if k == 0:
+                ad_quantise(3)
+            if k > 0:
+                wm_quantise(k - 1)
+                if k - 1 in last_period:
+                    pi = last_period[k - 1]
+                    todo.extend((pi, j) for j in range(2 * len(PANELS[pi])))
+            if k == n:
+                break
+            for lo, hi in plain_runs(k):
+                add_plain(nc.vector, k, lo, hi)
+            if k - 1 in BPREP:
+                b_quantise(BPREP[k - 1])
+            if k in BPREP:
+                b_widen(BPREP[k])
+                b_interleave(BPREP[k], nc.scalar.copy)
+            if k + 1 < n:
+                for u in range(4):
+                    first_product(k + 1, u)
+                for u in range(4):
+                    turn_back(k + 1, u)
+            for item in todo[:2]:
+                if open_item is not None:
+                    y_store(*open_item)
+                y_product(*item)
+                open_item = item
+            todo = todo[2:]
+        for item in todo:
+            if open_item is not None:
+                y_store(*open_item)
+            y_product(*item)
+            open_item = item
+        y_store(*open_item)

@@ -28,9 +28,9 @@ T_TILES = T // P
 FLOPS = 2 * IN * R * OUT + 2 * T * IN * OUT
 
 PANELS = [[0, 1], [2, 3], [4, 5, 6, 7], [8, 9], [10], [11]]
-PATTERNS = ["TTTT", "TTTT", "TTPP"] + ["TTPP", "PPTP"] * 4 + ["PPPP"]
+PATTERNS = ["TTTT","TTTP","TTTP","PPTP","TTTP","TTTT","PPPP","TTPP","PPPP","PPTP","PPPP","PPPP"]
 BPREP = {0: 1, 1: 2, 2: 3, 4: 4, 6: 5}
-DP, DT, TB, YB = 2, 2, 2, 2
+DP, DT, TB, YB = 2, 2, 1, 3
 HP = 64
 
 
@@ -41,7 +41,6 @@ def tile_vera_merged_layer_s13_kernel(tc, x_words, x_scales, a, bmat_bytes, bmat
         work = ctx.enter_context(tc.tile_pool(name="work", bufs=2))
         psum = ctx.enter_context(tc.psum_pool(name="psum", bufs=2))
 
-        d_row = keep.tile([P, R], BF16, name="d_row")
         b_row = keep.tile([P, OUT], BF16, name="b_row")
         ones = keep.tile([P, P], BF16, name="ones")
         warm = keep.tile([P, 8], F32, name="warm")
@@ -60,7 +59,7 @@ def tile_vera_merged_layer_s13_kernel(tc, x_words, x_scales, a, bmat_bytes, bmat
         w_pla = keep.tile([P, GROUPS * OUT], U8, name="w_pla", align_bytes=64)
         x_cod = keep.tile([P, GROUPS, 2 * T], U8, name="x_cod", align_bytes=64)
         x_pla = keep.tile([P, GROUPS, T], U8, name="x_pla", align_bytes=64)
-        dg = keep.tile([P, R], BF16, name="dg")
+        d_col = keep.tile([P, PACK], BF16, name="d_col")
         bg = keep.tile([P, OUT], F32, name="bg")
         b_col = keep.tile([P, BLOCKS], F32, name="b_col")
 
@@ -68,13 +67,11 @@ def tile_vera_merged_layer_s13_kernel(tc, x_words, x_scales, a, bmat_bytes, bmat
         w_view = w0.rearrange("(g p t) o -> g p t o", p=P, t=PACK)
         b_view = bmat_bytes.rearrange("(p t) o -> p t o", t=PACK)
 
-        nc.vector.memset(d_row[:], 0.0)
-        nc.scalar.dma_start(out=d_row[0:1, :], in_=d_gain.rearrange("(o r) -> o r", o=1))
+        nc.scalar.dma_start(out=d_col[:], in_=d_gain.rearrange("(p t) -> p t", t=PACK))
         nc.vector.memset(warm[:], 0.0)
         nc.scalar.activation(out=warm[:, 0:4], in_=warm[:, 4:8], func=COPY)
         nc.vector.memset(ones[:], 1.0)
         nc.gpsimd.memset(b_row[:], 0.0)
-        nc.scalar.dma_start(out=b_row[0:1, :], in_=b_gain.rearrange("(o r) -> o r", o=1))
         make_identity(nc, ident[:])
         nc.gpsimd.memset(x_pla[:].rearrange("p g n -> p (g n)").bitcast(U32), 0)
 
@@ -90,6 +87,7 @@ def tile_vera_merged_layer_s13_kernel(tc, x_words, x_scales, a, bmat_bytes, bmat
             cols = slice(c * CHUNK, (c + 1) * CHUNK)
             nc.sync.dma_start(out=w_raw[:, g, :, cols], in_=w_view[g][:, :, cols])
 
+        nc.sync.dma_start(out=b_row[0:1, :], in_=b_gain.rearrange("(o r) -> o r", o=1))
         load_a(1)
         load_w(0, 0)
         load_a(2)
@@ -112,25 +110,29 @@ def tile_vera_merged_layer_s13_kernel(tc, x_words, x_scales, a, bmat_bytes, bmat
         ad_tiles = {}
         grp_tiles = {}
 
-        def ad_product(g, h):
-            if h == 0:
-                ad_tiles[g] = work.tile([P, PACK, R], BF16, name="ad", tag="ad", align_bytes=64)
-            ts = slice(2 * h, 2 * h + 2)
-            nc.vector.tensor_tensor(
-                out=ad_tiles[g][:, ts, :], in0=a_raw[:, g, ts, :], in1=dg[:].unsqueeze(1).to_broadcast([P, 2, R]), op=MULT
-            )
-
         def ad_turn(g, h):
             if h == 0:
                 grp_tiles[g] = work.tile([P, P * PACK, PACK], BF16, name="ad_grp", tag="ad_grp", align_bytes=64)
-            bank = psum.tile([P, 2, 2, P], F32, name="bank_a", tag="y", bufs=YB)
-            for s in range(2):
-                words = ad_tiles[g][:, 2 * h + s, :].bitcast(F32)
+            bank = psum.tile([P, 2, HALF], F32, name="bank_a", tag="y", bufs=YB)
+            ad_tiles[(g, h)] = bank
+            if g >= 1:
+                turned_words = work.tile([P, 2, 2, P], F32, name="a_words", tag="a_words")
+                nc.scalar.copy(
+                    out=turned_words[:],
+                    in_=a_raw[:, g, 2 * h : 2 * h + 2, :].bitcast(F32).rearrange("p i (m u) -> p i u m", u=2),
+                )
+            for i in range(2):
+                words = a_raw[:, g, 2 * h + i, :].bitcast(F32)
                 for u in range(2):
-                    nc.tensor.transpose(bank[:, s, u, :], words[:, u::2], ident[:])
-            nc.scalar.copy(
-                out=grp_tiles[g][:, h * HALF : (h + 1) * HALF, :].bitcast(F32).rearrange("p (s i) u -> p s i u", s=2),
-                in_=bank[:].rearrange("p s u i -> p s i u"),
+                    in_words = turned_words[:, i, u, :] if g >= 1 else words[:, u::2]
+                    nc.tensor.transpose(bank[:, u, i * P : (i + 1) * P], in_words, ident[:])
+
+        def ad_product(g, h):
+            nc.vector.tensor_tensor(
+                out=grp_tiles[g][:, h * HALF : (h + 1) * HALF, :].rearrange("p n (u e) -> p n u e", u=2),
+                in0=ad_tiles[(g, h)][:].bitcast(BF16).rearrange("p u (n e) -> p n u e", e=2),
+                in1=d_col[:].rearrange("p (u e) -> p u e", u=2).unsqueeze(1).to_broadcast([P, HALF, 2, 2]),
+                op=MULT,
             )
 
         def ad_quantise(g):
@@ -289,50 +291,43 @@ def tile_vera_merged_layer_s13_kernel(tc, x_words, x_scales, a, bmat_bytes, bmat
                 engine(out=res[:], in_=y_banks[(pi, j)][:])
             nc.sync.dma_start(out=out_view[:, j * tiles : (j + 1) * tiles, o0 : o0 + width], in_=res[:])
 
-        def b_widen_v(k):
-            cols = slice(k * HALF, (k + 1) * HALF)
-            for t in range(PACK):
-                nc.vector.tensor_scalar(
-                    out=b_wide[:, t, cols], in0=b_raw[:, t, cols].bitcast(E4M3), scalar1=b_sc[:, t : t + 1], scalar2=None, op0=MULT
-                )
-
-        bank = psum.tile([P, R], F32, name="bank_g", tag="y", bufs=YB)
-        nc.tensor.matmul(bank[:], lhsT=ones[:], rhs=d_row[:], start=True, stop=True)
-        nc.scalar.copy(out=dg[:], in_=bank[:])
-        b_widen_v(0)
-        ad_product(0, 0)
-        ad_product(0, 1)
+        for i in range(0):
+            bank = psum.tile([P, R], F32, name="bank_w", tag="y", bufs=YB)
+            nc.tensor.matmul(bank[:], lhsT=ones[:], rhs=b_row[:, 0:R], start=True, stop=True)
+        b_widen(0)
         ad_turn(0, 0)
         ad_turn(0, 1)
-        bank = psum.tile([P, BLOCKS], F32, name="bank_c", tag="y", bufs=YB)
-        for ob in range(BLOCKS):
-            nc.tensor.matmul(bank[:, ob : ob + 1], lhsT=b_row[:, ob * P : (ob + 1) * P], rhs=ones[:, 0:1], start=True, stop=True)
-        b_interleave(0, nc.vector.tensor_copy)
-        ad_product(1, 0)
-        ad_product(1, 1)
-        b_quantise(0)
+        ad_product(0, 0)
+        ad_product(0, 1)
+        b_interleave(0, nc.scalar.copy)
         ad_quantise(0)
+        b_quantise(0)
         ad_turn(1, 0)
         ad_turn(1, 1)
+        bank = psum.tile([P, BLOCKS], F32, name="bank_c", tag="t", bufs=TB)
+        for ob in range(BLOCKS):
+            nc.tensor.matmul(bank[:, ob : ob + 1], lhsT=b_row[:, ob * P : (ob + 1) * P], rhs=ones[:, 0:1], start=True, stop=True)
         nc.scalar.copy(out=b_col[:], in_=bank[:])
+        ad_product(1, 0)
+        ad_product(1, 1)
         for u in range(2):
             first_product(0, u)
-        ad_product(2, 0)
-        ad_product(2, 1)
         for u in range(2):
             turn_back(0, u)
         ad_quantise(1)
         ad_turn(2, 0)
         ad_turn(2, 1)
+        ad_product(2, 0)
+        ad_product(2, 1)
         for u in range(2, 4):
             first_product(0, u)
         for u in range(2, 4):
             turn_back(0, u)
-        ad_product(3, 0)
-        ad_product(3, 1)
-        ad_quantise(2)
         ad_turn(3, 0)
         ad_turn(3, 1)
+        ad_quantise(2)
+        ad_product(3, 0)
+        ad_product(3, 1)
         for j in range(3):
             bank = psum.tile([P, CHUNK], F32, name="bank_b", tag="y", bufs=YB)
             nc.tensor.matmul(bank[:], lhsT=ones[:], rhs=b_row[:, j * CHUNK : (j + 1) * CHUNK], start=True, stop=True)
@@ -379,12 +374,12 @@ def tile_vera_merged_layer_s13_kernel(tc, x_words, x_scales, a, bmat_bytes, bmat
                     first_product(k + 1, u)
                 for u in range(4):
                     turn_back(k + 1, u)
-            for item in todo[:2]:
+            for item in todo[:1]:
                 if open_item is not None:
                     y_store(*open_item)
                 y_product(*item)
                 open_item = item
-            todo = todo[2:]
+            todo = todo[1:]
         for item in todo:
             if open_item is not None:
                 y_store(*open_item)

from contextlib import ExitStack

import concourse.mybir as mybir
from concourse.masks import make_identity

F32 = mybir.dt.float32
BF16 = mybir.dt.bfloat16
I32 = mybir.dt.int32
U32 = mybir.dt.uint32
U8 = mybir.dt.uint8
E4M3 = mybir.dt.float8_e4m3fn
E4M3X4 = mybir.dt.float8_e4m3fn_x4
E2M1X4 = mybir.dt.float4_e2m1fn_x4
MULT = mybir.AluOpType.mult
ADD = mybir.AluOpType.add
COPY = mybir.ActivationFunctionType.Copy

T, IN, R, OUT = 1024, 2048, 512, 1536
P = 128
PACK = 4
GROUPS = IN // (P * PACK)
CHUNK = 512
CHUNKS = OUT // CHUNK
HALF = 256
BLOCKS = OUT // P
T_TILES = T // P

FLOPS = 2 * IN * R * OUT + 2 * T * IN * OUT

PANELS = [[0, 1], [2, 3], [4, 5, 6, 7], [8, 9], [10], [11]]
PATTERNS = ["TTTT","TTTP","TTTP","PPTP","TTTP","TTTT","PPPP","TTPP","PPPP","PPTP","PPPP","PPPP"]
BPREP = {0: 1, 1: 2, 2: 3, 4: 4, 6: 5}
DP, DT, TB, YB = 2, 2, 1, 3
HP = 64


def tile_vera_merged_layer_s13_kernel(tc, x_words, x_scales, a, bmat_bytes, bmat_scale, d_gain, b_gain, w0, out):
    nc = tc.nc
    with ExitStack() as ctx:
        keep = ctx.enter_context(tc.tile_pool(name="keep", bufs=1))
        work = ctx.enter_context(tc.tile_pool(name="work", bufs=2))
        psum = ctx.enter_context(tc.psum_pool(name="psum", bufs=2))

        b_row = keep.tile([P, OUT], BF16, name="b_row")
        ones = keep.tile([P, P], BF16, name="ones")
        warm = keep.tile([P, 8], F32, name="warm")
        ident = keep.tile([P, P], F32, name="ident")
        b_sc = keep.tile([P, PACK], F32, name="b_sc")
        b_raw = keep.tile([P, PACK, OUT], U8, name="b_raw", align_bytes=64)
        b_wide = keep.tile([P, PACK, OUT], BF16, name="b_wide", align_bytes=64)
        b_grp = keep.tile([P, OUT, PACK], BF16, name="b_grp", align_bytes=64)
        b_cod = keep.tile([P, OUT], U32, name="b_cod", align_bytes=64)
        b_pla = keep.tile([P, OUT], U8, name="b_pla", align_bytes=64)
        a_raw = keep.tile([P, GROUPS, PACK, R], BF16, name="a_raw", align_bytes=64)
        a_cod = keep.tile([P, GROUPS, P * PACK], U32, name="a_cod", align_bytes=64)
        a_pla = keep.tile([P, GROUPS, P * PACK], U8, name="a_pla", align_bytes=64)
        w_raw = keep.tile([P, GROUPS, PACK, OUT], BF16, name="w_raw", align_bytes=64)
        w_cod = keep.tile([P, GROUPS * OUT], U32, name="w_cod", align_bytes=64)
        w_pla = keep.tile([P, GROUPS * OUT], U8, name="w_pla", align_bytes=64)
        x_cod = keep.tile([P, GROUPS, 2 * T], U8, name="x_cod", align_bytes=64)
        x_pla = keep.tile([P, GROUPS, T], U8, name="x_pla", align_bytes=64)
        d_col = keep.tile([P, PACK], BF16, name="d_col")
        bg = keep.tile([P, OUT], F32, name="bg")
        b_col = keep.tile([P, BLOCKS], F32, name="b_col")

        a_view = a.rearrange("(g p t) r -> g p t r", p=P, t=PACK)
        w_view = w0.rearrange("(g p t) o -> g p t o", p=P, t=PACK)
        b_view = bmat_bytes.rearrange("(p t) o -> p t o", t=PACK)

        nc.scalar.dma_start(out=d_col[:], in_=d_gain.rearrange("(p t) -> p t", t=PACK))
        nc.vector.memset(warm[:], 0.0)
        nc.scalar.activation(out=warm[:, 0:4], in_=warm[:, 4:8], func=COPY)
        nc.vector.memset(ones[:], 1.0)
        nc.gpsimd.memset(b_row[:], 0.0)
        make_identity(nc, ident[:])
        nc.gpsimd.memset(x_pla[:].rearrange("p g n -> p (g n)").bitcast(U32), 0)

        nc.sync.dma_start(out=b_sc[:], in_=bmat_scale.rearrange("(p t) o -> p (t o)", t=PACK))
        nc.sync.dma_start(out=b_raw[:, :, 0:CHUNK], in_=b_view[:, :, 0:CHUNK])
        for h in range(2):
            nc.sync.dma_start(out=a_raw[:, 0, 2 * h : 2 * h + 2, :], in_=a_view[0][:, 2 * h : 2 * h + 2, :])

        def load_a(g):
            nc.sync.dma_start(out=a_raw[:, g, :, :], in_=a_view[g])

        def load_w(c, g):
            cols = slice(c * CHUNK, (c + 1) * CHUNK)
            nc.sync.dma_start(out=w_raw[:, g, :, cols], in_=w_view[g][:, :, cols])

        nc.sync.dma_start(out=b_row[0:1, :], in_=b_gain.rearrange("(o r) -> o r", o=1))
        load_a(1)
        load_w(0, 0)
        load_a(2)
        load_w(0, 1)
        load_a(3)
        load_w(0, 2)
        load_w(0, 3)
        nc.sync.dma_start(out=b_raw[:, :, CHUNK:OUT], in_=b_view[:, :, CHUNK:OUT])
        for g in range(GROUPS):
            load_w(1, g)
        nc.sync.dma_start(out=x_cod[:].bitcast(I32), in_=x_words.bitcast(I32).rearrange("g p n -> p g n"))
        for q in range(4):
            nc.sync.dma_start(
                out=x_pla[32 * q : 32 * q + 4, :, :].bitcast(I32),
                in_=x_scales[:, 4 * q : 4 * q + 4, :].bitcast(I32).rearrange("g q n -> q g n"),
            )
        for g in range(GROUPS):
            load_w(2, g)

        ad_tiles = {}
        grp_tiles = {}

        def ad_turn(g, h):
            if h == 0:
                grp_tiles[g] = work.tile([P, P * PACK, PACK], BF16, name="ad_grp", tag="ad_grp", align_bytes=64)
            bank = psum.tile([P, 2, HALF], F32, name="bank_a", tag="y", bufs=YB)
            ad_tiles[(g, h)] = bank
            if g >= 1:
                turned_words = work.tile([P, 2, 2, P], F32, name="a_words", tag="a_words")
                nc.scalar.copy(
                    out=turned_words[:],
                    in_=a_raw[:, g, 2 * h : 2 * h + 2, :].bitcast(F32).rearrange("p i (m u) -> p i u m", u=2),
                )
            for i in range(2):
                words = a_raw[:, g, 2 * h + i, :].bitcast(F32)
                for u in range(2):
                    in_words = turned_words[:, i, u, :] if g >= 1 else words[:, u::2]
                    nc.tensor.transpose(bank[:, u, i * P : (i + 1) * P], in_words, ident[:])

        def ad_product(g, h):
            nc.vector.tensor_tensor(
                out=grp_tiles[g][:, h * HALF : (h + 1) * HALF, :].rearrange("p n (u e) -> p n u e", u=2),
                in0=ad_tiles[(g, h)][:].bitcast(BF16).rearrange("p u (n e) -> p n u e", e=2),
                in1=d_col[:].rearrange("p (u e) -> p u e", u=2).unsqueeze(1).to_broadcast([P, HALF, 2, 2]),
                op=MULT,
            )

        def ad_quantise(g):
            nc.vector.quantize_mx(
                out=a_cod[:, g, :].bitcast(E4M3X4), scales=a_pla[:, g, :], in_=grp_tiles[g][:].rearrange("p n t -> p (n t)")
            )

        def b_widen(k):
            cols = slice(k * HALF, (k + 1) * HALF)
            for t in range(PACK):
                nc.scalar.activation(out=b_wide[:, t, cols], in_=b_raw[:, t, cols].bitcast(E4M3), func=COPY, scale=b_sc[:, t : t + 1])

        def b_interleave(k, copy):
            cols = slice(k * HALF, (k + 1) * HALF)
            copy(out=b_grp[:, cols, :], in_=b_wide[:, :, cols].rearrange("p t c -> p c t"))

        def b_quantise(k):
            cols = slice(k * HALF, (k + 1) * HALF)
            nc.vector.quantize_mx(
                out=b_cod[:, cols].bitcast(E4M3X4), scales=b_pla[:, cols], in_=b_grp[:, cols, :].rearrange("p c t -> p (c t)")
            )

        periods = []
        last_period = {}
        bases = {}
        base = 0
        for pi, panel in enumerate(PANELS):
            bases[pi] = base
            order = [(g, ob) for g in range(GROUPS) for ob in panel]
            for i in range(0, len(order), 4):
                periods.append((order[i : i + 4], base + i * P, PATTERNS[len(periods)]))
            last_period[len(periods) - 1] = pi
            base += GROUPS * len(panel) * P
        banks, scaled, turned, prods, wm = {}, {}, {}, {}, {}

        def first_product(k, u):
            (g, ob), kind = periods[k][0][u], periods[k][2][u]
            cols = slice(ob * P, (ob + 1) * P)
            bank = psum.tile([P, PACK, P], F32, name="bank_d", tag="dt" if kind == "T" else "dp", bufs=DT if kind == "T" else DP)
            banks[(k, u)] = bank
            if kind == "T":
                nc.tensor.matmul_mx(
                    out=bank[:].rearrange("p t o -> p (t o)"),
                    lhsT=b_cod[:, cols].bitcast(E4M3X4),
                    lhsT_scale=b_pla[:, cols],
                    rhs=a_cod[:, g, :].bitcast(E4M3X4),
                    rhs_scale=a_pla[:, g, :],
                    start=True,
                    stop=True,
                )
                tile = work.tile([P, PACK, P], F32, name="scaled", tag="scaled", bufs=6)
                scaled[(k, u)] = tile
                nc.scalar.activation(out=tile[:], in_=bank[:], func=COPY, scale=b_col[:, ob : ob + 1])
            else:
                for t in range(PACK):
                    nc.tensor.matmul_mx(
                        out=bank[:, t, :],
                        lhsT=a_cod[:, g, t * P : (t + 1) * P].bitcast(E4M3X4),
                        lhsT_scale=a_pla[:, g, t * P : (t + 1) * P],
                        rhs=b_cod[:, cols].bitcast(E4M3X4),
                        rhs_scale=b_pla[:, cols],
                        start=True,
                        stop=True,
                    )

        def turn_back(k, u):
            if periods[k][2][u] == "T":
                bank = psum.tile([P, PACK, P], F32, name="bank_t", tag="t", bufs=TB)
                turned[(k, u)] = bank
                for t in range(PACK):
                    nc.tensor.transpose(bank[:, t, :], scaled[(k, u)][:, t, :], ident[:])

        def scale_plain(k, u):
            g, ob = periods[k][0][u]
            nc.vector.tensor_tensor(
                out=prods[k][:, u * P : (u + 1) * P, :],
                in0=banks[(k, u)][:].rearrange("p t o -> p o t"),
                in1=bg[:, ob * P : (ob + 1) * P].unsqueeze(2).to_broadcast([P, P, PACK]),
                op=MULT,
            )

        def add_turned(k, u):
            g, ob = periods[k][0][u]
            nc.vector.tensor_tensor(
                out=wm[k][:, u * P : (u + 1) * P, :],
                in0=turned[(k, u)][:].rearrange("p t o -> p o t"),
                in1=w_raw[:, g, :, ob * P : (ob + 1) * P].rearrange("p t o -> p o t"),
                op=ADD,
            )

        def add_plain(engine, k, lo, hi):
            g, ob = periods[k][0][lo // P]
            o0 = ob * P + lo % P
            engine.tensor_tensor(
                out=wm[k][:, lo:hi, :],
                in0=prods[k][:, lo:hi, :],
                in1=w_raw[:, g, :, o0 : o0 + hi - lo].rearrange("p t o -> p o t"),
                op=ADD,
            )

        def plain_runs(k):
            units, at, pattern = periods[k]
            runs = []
            for u in range(4):
                if pattern[u] not in "Pg":
                    continue
                lo = u * P + (HP if pattern[u] == "g" else 0)
                hi = (u + 1) * P
                if runs and runs[-1][1] == lo and units[u][0] == units[u - 1][0]:
                    runs[-1][1] = hi
                else:
                    runs.append([lo, hi])
            return runs

        def wm_quantise(k, lo=0, hi=4 * P):
            at = periods[k][1]
            nc.vector.quantize_mx(
                out=w_cod[:, at + lo : at + hi].bitcast(E4M3X4),
                scales=w_pla[:, at + lo : at + hi],
                in_=wm[k][:, lo:hi, :].rearrange("p o t -> p (o t)"),
            )

        y_banks = {}

        def y_product(pi, j):
            width = len(PANELS[pi]) * P
            n = min(width, CHUNK) if width == CHUNK else P
            tiles = CHUNK // width
            bank = psum.tile([P, tiles, width], F32, name="bank_y", tag="y", bufs=YB)
            y_banks[(pi, j)] = bank
            for i in range(tiles):
                tt = j * tiles + i
                for o in range(0, width, n):
                    for g in range(GROUPS):
                        at = bases[pi] + g * width + o
                        nc.tensor.matmul_mx(
                            out=bank[:, i, o : o + n],
                            lhsT=x_cod[:, g, tt * 2 * P : (tt + 1) * 2 * P].bitcast(E2M1X4),
                            lhsT_scale=x_pla[:, g, tt * P : (tt + 1) * P],
                            rhs=w_cod[:, at : at + n].bitcast(E4M3X4),
                            rhs_scale=w_pla[:, at : at + n],
                            start=g == 0,
                            stop=g == GROUPS - 1,
                        )

        out_view = out.rearrange("(m p) o -> p m o", p=P)

        def y_store(pi, j, engine=None):
            width = len(PANELS[pi]) * P
            tiles = CHUNK // width
            o0 = PANELS[pi][0] * P
            res = work.tile([P, tiles, width], F32, name="res", tag="res", bufs=6)
            if engine is None:
                nc.scalar.copy(out=res[:], in_=y_banks[(pi, j)][:])
            else:
                engine(out=res[:], in_=y_banks[(pi, j)][:])
            nc.sync.dma_start(out=out_view[:, j * tiles : (j + 1) * tiles, o0 : o0 + width], in_=res[:])

        for i in range(0):
            bank = psum.tile([P, R], F32, name="bank_w", tag="y", bufs=YB)
            nc.tensor.matmul(bank[:], lhsT=ones[:], rhs=b_row[:, 0:R], start=True, stop=True)
        b_widen(0)
        ad_turn(0, 0)
        ad_turn(0, 1)
        ad_product(0, 0)
        ad_product(0, 1)
        b_interleave(0, nc.scalar.copy)
        ad_quantise(0)
        b_quantise(0)
        ad_turn(1, 0)
        ad_turn(1, 1)
        bank = psum.tile([P, BLOCKS], F32, name="bank_c", tag="t", bufs=TB)
        for ob in range(BLOCKS):
            nc.tensor.matmul(bank[:, ob : ob + 1], lhsT=b_row[:, ob * P : (ob + 1) * P], rhs=ones[:, 0:1], start=True, stop=True)
        nc.scalar.copy(out=b_col[:], in_=bank[:])
        ad_product(1, 0)
        ad_product(1, 1)
        for u in range(2):
            first_product(0, u)
        for u in range(2):
            turn_back(0, u)
        ad_quantise(1)
        ad_turn(2, 0)
        ad_turn(2, 1)
        ad_product(2, 0)
        ad_product(2, 1)
        for u in range(2, 4):
            first_product(0, u)
        for u in range(2, 4):
            turn_back(0, u)
        ad_turn(3, 0)
        ad_turn(3, 1)
        ad_quantise(2)
        ad_product(3, 0)
        ad_product(3, 1)
        for j in range(3):
            bank = psum.tile([P, CHUNK], F32, name="bank_b", tag="y", bufs=YB)
            nc.tensor.matmul(bank[:], lhsT=ones[:], rhs=b_row[:, j * CHUNK : (j + 1) * CHUNK], start=True, stop=True)
            nc.scalar.copy(out=bg[:, j * CHUNK : (j + 1) * CHUNK], in_=bank[:])

        n = len(periods)
        todo = []
        open_item = None
        for k in range(n + 1):
            if k < n:
                units, at, pattern = periods[k]
                prods[k] = work.tile([P, 4 * P, PACK], F32, name="prod", tag="prod", bufs=2)
                wm[k] = work.tile([P, 4 * P, PACK], BF16, name="wm", tag="wm", bufs=3, align_bytes=64)
                for kind in "GgP":
                    for u in range(4):
                        if pattern[u] == kind:
                            scale_plain(k, u)
                for u in range(4):
                    if pattern[u] == "G":
                        add_plain(nc.gpsimd, k, u * P, (u + 1) * P)
                    if pattern[u] == "g":
                        add_plain(nc.gpsimd, k, u * P, u * P + HP)
                for u in range(4):
                    if pattern[u] == "T":
                        add_turned(k, u)
            if k == 0:
                ad_quantise(3)
            if k > 0:
                wm_quantise(k - 1)
                if k - 1 in last_period:
                    pi = last_period[k - 1]
                    todo.extend((pi, j) for j in range(2 * len(PANELS[pi])))
            if k == n:
                break
            for lo, hi in plain_runs(k):
                add_plain(nc.vector, k, lo, hi)
            if k - 1 in BPREP:
                b_quantise(BPREP[k - 1])
            if k in BPREP:
                b_widen(BPREP[k])
                b_interleave(BPREP[k], nc.scalar.copy)
            if k + 1 < n:
                for u in range(4):
                    first_product(k + 1, u)
                for u in range(4):
                    turn_back(k + 1, u)
            for item in todo[:1]:
                if open_item is not None:
                    y_store(*open_item)
                y_product(*item)
                open_item = item
            todo = todo[1:]
        for item in todo:
            if open_item is not None:
                y_store(*open_item)
            y_product(*item)
            open_item = item
        y_store(*open_item)
